import numpy as np
import ml_dtypes


def mxq(x, axis, fmt="e4m3"):
    dtype, down = {"e4m3": (ml_dtypes.float8_e4m3fn, 7), "e5m2": (ml_dtypes.float8_e5m2, 14)}[fmt]
    v = np.moveaxis(np.asarray(x, np.float32).astype(ml_dtypes.bfloat16).astype(np.float64), axis, -1)
    blocks = v.reshape(v.shape[:-1] + (-1, 32))
    amax = np.abs(blocks).max(-1, keepdims=True)
    byte = np.maximum(np.where(amax > 0, np.frexp(amax)[1] - 1 + 127, 0) - down, 1)
    scale = np.exp2(byte - 127.0)
    codes = (blocks / scale).astype(np.float32).astype(dtype).astype(np.float64)
    return np.moveaxis((codes * scale).reshape(v.shape), -1, axis)


WIDE = False


def mx_kscale(k):
    if not WIDE:
        return np.ones(k)
    levels = np.array([10, -10, 5, -5, 0])
    if k % 512:
        return np.exp2(np.random.permutation(np.resize(levels, k // 32))).repeat(32)
    a = np.empty((k // 512, 16))
    for p in range(k // 512):
        a[p, :8] = np.random.permutation(np.resize(levels, 8))
        for g in range(8):
            far = levels[np.abs(levels - a[p, g]) >= 10]
            a[p, g + 8] = far[np.random.randint(len(far))]
    return np.exp2(a.ravel()).repeat(32)


def f64(x):
    return np.asarray(x).astype(np.float64)


def striped(idx):
    return np.tile(np.asarray(idx).reshape(-1, 16).T, (8, 1)).astype(np.uint16)


def unstriped(offs):
    return offs[:16].T.reshape(-1).astype(np.int64)


E2M1 = np.array([0.0, 0.5, 1.0, 1.5, 2.0, 3.0, 4.0, 6.0, -0.0, -0.5, -1.0, -1.5, -2.0, -3.0, -4.0, -6.0])


def pack_weight(w, fmt):
    k, n = w.shape
    w = f64(np.asarray(w, np.float32).astype(ml_dtypes.bfloat16)).reshape(k // 32, 32, n)
    amax = np.abs(w).max(1)
    if fmt == "e4m3":
        byte = np.frexp(amax)[1] - 1 + 127 - 7
    else:
        mant, ex = np.frexp(amax / 6.0)
        byte = np.where(mant > 0.5, ex, ex - 1) + 127
    byte = np.clip(np.where(amax > 0, byte, 1), 1, 254)
    scaled = (w * np.exp2(127.0 - byte)[:, None, :]).reshape(k, n).astype(np.float32)
    by_word = np.ascontiguousarray(scaled.reshape(k // 512, 128, 4, n).transpose(0, 1, 3, 2))
    if fmt == "e4m3":
        words = by_word.astype(ml_dtypes.float8_e4m3fn).view(np.uint8)
    else:
        c = by_word.astype(ml_dtypes.float4_e2m1fn).view(np.uint8) & 0xF
        words = (c[..., 0::2] | (c[..., 1::2] << 4)).reshape(k // 512, 128, 2 * n)
    return np.ascontiguousarray(words), np.ascontiguousarray(byte.astype(np.uint8).reshape(k // 512, 16, n))


def unpack_weight(words, scales, fmt):
    g, _, n = scales.shape
    words = np.ascontiguousarray(words).reshape(g, 128, n, -1)
    if fmt == "e4m3":
        vals = words.view(ml_dtypes.float8_e4m3fn).astype(np.float64)
    else:
        nib = np.empty((g, 128, n, 4), np.uint8)
        nib[..., 0::2] = words & 0xF
        nib[..., 1::2] = words >> 4
        vals = E2M1[nib]
    vals = vals * np.repeat(np.exp2(scales.astype(np.float64) - 127.0), 8, axis=1)[..., None]
    return vals.transpose(0, 1, 3, 2).reshape(g * 512, n)


D, T, I, Q, E, J = 512, 2048, 512, 256, 512, 512


def setup_inputs():
    n = np.random.standard_normal
    idx = np.random.permutation(T)[:I]
    fd = mx_kscale(D)
    fi = mx_kscale(I)
    fj = mx_kscale(J)
    keysp = pack_weight(n((D, T)) / fd[:, None], "e4m3")
    return {
        "query": (n((D, Q)) * 1.0 / np.sqrt(D) * fd[:, None]).astype(np.float32),
        "keys_words": keysp[0],
        "keys_scales": keysp[1],
        "inv": (n((I, J)) * 1 / np.sqrt(I) * fi[:, None] / fj).astype(np.float32),
        "gain": (np.random.uniform(8.0, 24.0, (1, I)) / fi).astype(np.float32),
        "read": (n((J, E)) * fj[:, None]).astype(np.float32),
        "res": (n((Q, E)) * 4.0).astype(np.float32),
        "offs": striped(idx),
    }


def reference(query, keys_words, keys_scales, inv, gain, read, res, offs):
    idx = unstriped(offs)
    keysu = unpack_weight(keys_words, keys_scales, "e4m3")
    queryq = mxq(f64(query), 0, "e4m3")
    keysidxg = keysu[:, idx]
    a = queryq.T @ keysidxg
    p = np.exp(a - np.max(a, axis=1, keepdims=True))
    f = p / np.sum(p, axis=1, keepdims=True) * f64(gain)
    ft = f.T
    invq = mxq(f64(inv), 0, "e4m3")
    ftq = mxq(ft, 0, "e4m3")
    g = invq.T @ ftq
    gq = mxq(g, 0, "e4m3")
    readq = mxq(f64(read), 0, "e4m3")
    b = gq.T @ readq
    y = b + f64(res)
    return y

@@ -1,0 +1,196 @@
+from contextlib import ExitStack
+
+import concourse.mybir as mybir
+from concourse.masks import make_identity
+
+D, T, I, Q, E, J = 512, 2048, 512, 256, 512, 512
+FLOPS = 2 * Q * (D * I + I * J + J * E)
+
+F32 = mybir.dt.float32
+BF16 = mybir.dt.bfloat16
+I32 = mybir.dt.int32
+U32 = mybir.dt.uint32
+U16 = mybir.dt.uint16
+U8 = mybir.dt.uint8
+FP8X4 = mybir.dt.float8_e4m3fn_x4
+ALU = mybir.AluOpType
+ACT = mybir.ActivationFunctionType
+AXIS_X = mybir.AxisListType.X
+
+P = 128
+PACK = 4
+HALF = 256
+Q_TILES = Q // P
+
+
+def tile_attend_nystrom_kernel(tc, query, keys_words, keys_scales, inv, gain, read, res, offs, out):
+    nc = tc.nc
+
+    with ExitStack() as ctx:
+        keep = ctx.enter_context(tc.tile_pool(name="keep", bufs=1))
+        psum = ctx.enter_context(tc.psum_pool(name="psum", bufs=1))
+
+        def sb(name, shape, dtype):
+            return keep.tile(shape, dtype, name=name, align_bytes=64)
+
+        def quantize(name, grouped, width):
+            codes = sb(name + "_codes", [P, width], U32)
+            scales = sb(name + "_scales", [P, width], U8)
+            nc.vector.quantize_mx(out=codes[:].bitcast(FP8X4), scales=scales[:], in_=grouped)
+            return codes, scales
+
+        def mx(dst, stat, stat_cols, mov, mov_cols):
+            nc.tensor.matmul_mx(
+                out=dst,
+                lhsT=stat[0][:, stat_cols].bitcast(FP8X4),
+                lhsT_scale=stat[1][:, stat_cols],
+                rhs=mov[0][:, mov_cols].bitcast(FP8X4),
+                rhs_scale=mov[1][:, mov_cols],
+                start=True,
+                stop=True,
+            )
+
+        offsets = keep.tile([P, I // 16], U16, name="offsets")
+        nc.sync.dma_start(offsets[:], offs)
+
+        query_raw = sb("query_raw", [P, PACK, Q], F32)
+        nc.sync.dma_start(out=query_raw[:], in_=query.rearrange("(p t) q -> p t q", t=PACK))
+        pool_scales = sb("pool_scales", [P, T], U8)
+        nc.vector.memset(pool_scales[:].bitcast(I32), 0)
+        for quad in range(4):
+            nc.sync.dma_start(
+                out=pool_scales[32 * quad : 32 * quad + 4, :].bitcast(I32),
+                in_=keys_scales[0, 4 * quad : 4 * quad + 4, :].bitcast(I32),
+            )
+
+        pool_words = sb("pool_words", [P, T], U32)
+        nc.sync.dma_start(
+            out=pool_words[:].bitcast(I32),
+            in_=keys_words[0].rearrange("p n t -> p (n t)").bitcast(I32),
+        )
+        gain_cols = sb("gain_cols", [P, PACK], F32)
+        nc.scalar.dma_start(out=gain_cols[:], in_=gain.rearrange("o (s r) -> (o s) r", r=PACK))
+
+        inv_rows = inv.rearrange("(p t) j -> p t j", t=PACK)
+        read_rows = read.rearrange("(p t) e -> p t e", t=PACK)
+        inv_raw, read_raw, res_sb = [], [], []
+        for h in range(2):
+            tile = sb(f"inv_raw{h}", [P, PACK, HALF], F32)
+            nc.sync.dma_start(out=tile[:], in_=inv_rows[:, :, h * HALF : (h + 1) * HALF])
+            inv_raw.append(tile)
+        for h in range(2):
+            tile = sb(f"read_raw{h}", [P, PACK, HALF], F32)
+            nc.sync.dma_start(out=tile[:], in_=read_rows[:, :, h * HALF : (h + 1) * HALF])
+            read_raw.append(tile)
+        for n in range(Q_TILES):
+            tile = sb(f"res{n}", [P, E], F32)
+            nc.sync.dma_start(out=tile[:], in_=res[n * P : (n + 1) * P, :])
+            res_sb.append(tile)
+
+        ident = sb("ident", [P, P], F32)
+        make_identity(nc, ident[:])
+
+        query_grouped = [sb(f"query_grouped{n}", [P, P, PACK], BF16) for n in range(Q_TILES)]
+        nc.vector.tensor_copy(out=query_grouped[0][:], in_=query_raw[:, :, 0:P].rearrange("p t q -> p q t"))
+        nc.scalar.activation(
+            out=query_grouped[1][:], in_=query_raw[:, :, P : 2 * P].rearrange("p t q -> p q t"), func=ACT.Copy
+        )
+        key_scales = sb("key_scales", [P, I], U8)
+        nc.vector.tensor_copy(key_scales[:], pool_scales[:].indirect(offsets[:]))
+        query_mx = [
+            quantize(f"query{n}", query_grouped[n][:].rearrange("p q t -> p (q t)"), P) for n in range(Q_TILES)
+        ]
+
+        gain_bank = psum.tile([P, PACK, P], F32, name="gain_bank")
+        for r in range(PACK):
+            nc.tensor.transpose(gain_bank[:, r, :], gain_cols[:, r : r + 1].to_broadcast([P, P]), ident[:])
+        gain_wide = sb("gain_wide", [P, 2, P, 2], F32)
+        nc.scalar.copy(out=gain_wide[:], in_=gain_bank[:].rearrange("p (u e) s -> p u s e", e=2))
+
+        key_words = sb("key_words", [P, I], U32)
+        for h in range(2):
+            nc.vector.tensor_copy(
+                key_words[:, h * HALF : (h + 1) * HALF],
+                pool_words[:].indirect(offsets[:, h * (HALF // 16) : (h + 1) * (HALF // 16)]),
+            )
+        keys_mx = (key_words, key_scales)
+
+        scores = [psum.tile([P, I], F32, name=f"scores{n}") for n in range(Q_TILES)]
+        for n in range(Q_TILES):
+            for h in range(2):
+                cols = slice(h * HALF, (h + 1) * HALF)
+                mx(scores[n][:, cols], query_mx[n], slice(0, P), keys_mx, cols)
+
+        neg_max = [sb(f"neg_max{n}", [P, 1], F32) for n in range(Q_TILES)]
+        row_sum = [sb(f"row_sum{n}", [P, 1], F32) for n in range(Q_TILES)]
+        row_rcp = [sb(f"row_rcp{n}", [P, 1], F32) for n in range(Q_TILES)]
+        probs = [sb(f"probs{n}", [P, I], F32) for n in range(Q_TILES)]
+        for n in range(Q_TILES):
+            nc.vector.tensor_reduce(out=neg_max[n][:], in_=scores[n][:], axis=AXIS_X, op=ALU.max, negate=True)
+        for n in range(Q_TILES):
+            nc.scalar.activation(
+                out=probs[n][:].rearrange("p (u s e) -> p u s e", u=2, e=2),
+                in_=scores[n][:].rearrange("p (s u e) -> p u s e", u=2, e=2),
+                func=ACT.Exp,
+                bias=neg_max[n][:],
+                accum_out=row_sum[n][:],
+            )
+
+        inv_grouped = sb("inv_grouped", [P, PACK, P, PACK], BF16)
+        half_m = HALF // PACK
+        nc.scalar.copy(
+            out=inv_grouped[:, :, 0:half_m, :].rearrange("p t m r -> p m t r"),
+            in_=inv_raw[0][:].rearrange("p r (m t) -> p m t r", t=PACK),
+        )
+        nc.vector.tensor_copy(
+            out=inv_grouped[:, :, half_m : 2 * half_m, :].rearrange("p t m r -> p m t r"),
+            in_=inv_raw[1][:].rearrange("p r (m t) -> p m t r", t=PACK),
+        )
+
+        weights = [sb(f"weights{n}", [P, I], BF16) for n in range(Q_TILES)]
+        for n in range(Q_TILES):
+            nc.vector.reciprocal(out=row_rcp[n][:], in_=row_sum[n][:])
+            nc.vector.scalar_tensor_tensor(
+                out=weights[n][:],
+                in0=probs[n][:],
+                scalar=row_rcp[n][:],
+                in1=gain_wide[:].rearrange("p u s e -> p (u s e)"),
+                op0=ALU.mult,
+                op1=ALU.mult,
+            )
+        inv_mx = quantize("inv", inv_grouped[:].rearrange("p t m r -> p (t m r)"), J)
+
+        turned = [psum.tile([P, 2, P], F32, name=f"turned{n}") for n in range(Q_TILES)]
+        ft_grouped = [sb(f"ft_grouped{n}", [P, P * PACK], BF16) for n in range(Q_TILES)]
+        for n in range(Q_TILES):
+            pairs = weights[n][:].bitcast(F32)
+            for u in range(2):
+                nc.tensor.transpose(turned[n][:, u, :], pairs[:, u * P : (u + 1) * P], ident[:])
+            nc.scalar.copy(
+                out=ft_grouped[n][:].bitcast(F32).rearrange("p (q u) -> p q u", u=2),
+                in_=turned[n][:].rearrange("p u q -> p q u"),
+            )
+        ft_mx = [quantize(f"ft{n}", ft_grouped[n][:], P) for n in range(Q_TILES)]
+
+        read_grouped = [sb(f"read_grouped{h}", [P, HALF, PACK], BF16) for h in range(2)]
+        nc.scalar.copy(out=read_grouped[0][:], in_=read_raw[0][:].rearrange("p t e -> p e t"))
+        nc.vector.tensor_copy(out=read_grouped[1][:], in_=read_raw[1][:].rearrange("p t e -> p e t"))
+
+        g_grouped = [sb(f"g_grouped{n}", [P, P, PACK], BF16) for n in range(Q_TILES)]
+        for n in range(Q_TILES):
+            g_bank = psum.tile([P, PACK, P], F32, name=f"scores{n}")
+            for t in range(PACK):
+                mx(g_bank[:, t, :], inv_mx, slice(t * P, (t + 1) * P), ft_mx[n], slice(0, P))
+            nc.scalar.copy(out=g_grouped[n][:], in_=g_bank[:].rearrange("p t q -> p q t"))
+        read_mx = [
+            quantize(f"read{h}", read_grouped[h][:].rearrange("p e t -> p (e t)"), HALF) for h in range(2)
+        ]
+        for n in range(Q_TILES):
+            g_mx = quantize(f"g{n}", g_grouped[n][:].rearrange("p q t -> p (q t)"), P)
+            b_bank = psum.tile([P, E], F32, name=f"b_bank{n}")
+            for h in range(2):
+                cols = slice(h * HALF, (h + 1) * HALF)
+                mx(b_bank[:, cols], g_mx, slice(0, P), read_mx[h], slice(0, HALF))
+            result = sb(f"result{n}", [P, E], F32)
+            nc.vector.tensor_tensor(out=result[:], in0=b_bank[:], in1=res_sb[n][:], op=ALU.add)
+            nc.sync.dma_start(out=out[n * P : (n + 1) * P, :], in_=result[:])

@@ -30,13 +30,18 @@ def tile_attend_nystrom_kernel(tc, query, keys_words, keys_scales, inv, gain, re
         keep = ctx.enter_context(tc.tile_pool(name="keep", bufs=1))
         psum = ctx.enter_context(tc.psum_pool(name="psum", bufs=1))
 
-        def sb(name, shape, dtype):
-            return keep.tile(shape, dtype, name=name, align_bytes=64)
+        def sb(name, shape, dtype, tag=None):
+            return keep.tile(shape, dtype, name=name, tag=tag or name, align_bytes=64)
 
         def quantize(name, grouped, width):
             codes = sb(name + "_codes", [P, width], U32)
             scales = sb(name + "_scales", [P, width], U8)
-            nc.vector.quantize_mx(out=codes[:].bitcast(FP8X4), scales=scales[:], in_=grouped)
+            for c in range(0, width, P):
+                nc.vector.quantize_mx(
+                    out=codes[:, c : c + P].bitcast(FP8X4),
+                    scales=scales[:, c : c + P],
+                    in_=grouped[:, PACK * c : PACK * (c + P)],
+                )
             return codes, scales
 
         def mx(dst, stat, stat_cols, mov, mov_cols):
@@ -52,145 +57,167 @@ def tile_attend_nystrom_kernel(tc, query, keys_words, keys_scales, inv, gain, re
 
         offsets = keep.tile([P, I // 16], U16, name="offsets")
         nc.sync.dma_start(offsets[:], offs)
-
-        query_raw = sb("query_raw", [P, PACK, Q], F32)
-        nc.sync.dma_start(out=query_raw[:], in_=query.rearrange("(p t) q -> p t q", t=PACK))
-        pool_scales = sb("pool_scales", [P, T], U8)
-        nc.vector.memset(pool_scales[:].bitcast(I32), 0)
-        for quad in range(4):
-            nc.sync.dma_start(
-                out=pool_scales[32 * quad : 32 * quad + 4, :].bitcast(I32),
-                in_=keys_scales[0, 4 * quad : 4 * quad + 4, :].bitcast(I32),
-            )
-
-        pool_words = sb("pool_words", [P, T], U32)
-        nc.sync.dma_start(
-            out=pool_words[:].bitcast(I32),
-            in_=keys_words[0].rearrange("p n t -> p (n t)").bitcast(I32),
-        )
         gain_cols = sb("gain_cols", [P, PACK], F32)
         nc.scalar.dma_start(out=gain_cols[:], in_=gain.rearrange("o (s r) -> (o s) r", r=PACK))
 
-        inv_rows = inv.rearrange("(p t) j -> p t j", t=PACK)
-        read_rows = read.rearrange("(p t) e -> p t e", t=PACK)
-        inv_raw, read_raw, res_sb = [], [], []
-        for h in range(2):
-            tile = sb(f"inv_raw{h}", [P, PACK, HALF], F32)
-            nc.sync.dma_start(out=tile[:], in_=inv_rows[:, :, h * HALF : (h + 1) * HALF])
-            inv_raw.append(tile)
-        for h in range(2):
-            tile = sb(f"read_raw{h}", [P, PACK, HALF], F32)
-            nc.sync.dma_start(out=tile[:], in_=read_rows[:, :, h * HALF : (h + 1) * HALF])
-            read_raw.append(tile)
+        word_rows = keys_words[0].rearrange("p n t -> p (n t)").bitcast(I32)
+
+        def load_rows(name, matrix):
+            tile = sb(name, [P, PACK, matrix.shape[1]], F32)
+            nc.sync.dma_start(out=tile[:], in_=matrix.rearrange("(p t) c -> p t c", t=PACK))
+            return tile
+
+        pool_words = sb("pool_words", [P, T], U32)
+        pool_scales = sb("pool_scales", [P, T], U8)
+        ident = sb("ident", [P, P], F32)
+        nc.vector.memset(pool_scales[:].bitcast(I32), 0)
+        make_identity(nc, ident[:])
+
+        query_raw = load_rows("query_raw", query)
+        scale_rows = keys_scales[0].rearrange("(c f) n -> f c n", f=4)
+        for f in range(4):
+            nc.sync.dma_start(out=pool_scales[f:P:32, :].bitcast(I32), in_=scale_rows[f].bitcast(I32))
+        nc.sync.dma_start(out=pool_words[:].bitcast(I32), in_=word_rows)
+        inv_raw = load_rows("inv_raw", inv)
+        read_raw = load_rows("read_raw", read)
+        res_sb = []
         for n in range(Q_TILES):
             tile = sb(f"res{n}", [P, E], F32)
             nc.sync.dma_start(out=tile[:], in_=res[n * P : (n + 1) * P, :])
             res_sb.append(tile)
 
-        ident = sb("ident", [P, P], F32)
-        make_identity(nc, ident[:])
-
-        query_grouped = [sb(f"query_grouped{n}", [P, P, PACK], BF16) for n in range(Q_TILES)]
-        nc.vector.tensor_copy(out=query_grouped[0][:], in_=query_raw[:, :, 0:P].rearrange("p t q -> p q t"))
-        nc.scalar.activation(
-            out=query_grouped[1][:], in_=query_raw[:, :, P : 2 * P].rearrange("p t q -> p q t"), func=ACT.Copy
-        )
-        key_scales = sb("key_scales", [P, I], U8)
-        nc.vector.tensor_copy(key_scales[:], pool_scales[:].indirect(offsets[:]))
-        query_mx = [
-            quantize(f"query{n}", query_grouped[n][:].rearrange("p q t -> p (q t)"), P) for n in range(Q_TILES)
-        ]
-
         gain_bank = psum.tile([P, PACK, P], F32, name="gain_bank")
         for r in range(PACK):
             nc.tensor.transpose(gain_bank[:, r, :], gain_cols[:, r : r + 1].to_broadcast([P, P]), ident[:])
-        gain_wide = sb("gain_wide", [P, 2, P, 2], F32)
-        nc.scalar.copy(out=gain_wide[:], in_=gain_bank[:].rearrange("p (u e) s -> p u s e", e=2))
 
-        key_words = sb("key_words", [P, I], U32)
+        query_grouped = [sb("query_grouped0", [P, P, PACK], BF16), sb("query_grouped1", [P, P, PACK], BF16)]
+        nc.vector.tensor_copy(out=query_grouped[0][:], in_=query_raw[:, :, 0:P].rearrange("p t q -> p q t"))
+        nc.scalar.activation(out=query_grouped[1][:], in_=query_raw[:, :, P:Q].rearrange("p t q -> p q t"), func=ACT.Copy)
+        key_scales = sb("key_scales", [P, I], U8)
+        nc.vector.tensor_copy(key_scales[:], pool_scales[:].indirect(offsets[:]))
+        query_mx = [quantize("query0", query_grouped[0][:].rearrange("p q t -> p (q t)"), P)]
+        key_words = [sb(f"key_words{h}", [P, HALF], U32) for h in range(2)]
         for h in range(2):
             nc.vector.tensor_copy(
-                key_words[:, h * HALF : (h + 1) * HALF],
+                key_words[h][:],
                 pool_words[:].indirect(offsets[:, h * (HALF // 16) : (h + 1) * (HALF // 16)]),
             )
-        keys_mx = (key_words, key_scales)
+        keys_mx = [(key_words[h], key_scales[:, h * HALF : (h + 1) * HALF]) for h in range(2)]
+        query_mx.append(quantize("query1", query_grouped[1][:].rearrange("p q t -> p (q t)"), P))
 
-        scores = [psum.tile([P, I], F32, name=f"scores{n}") for n in range(Q_TILES)]
-        for n in range(Q_TILES):
-            for h in range(2):
-                cols = slice(h * HALF, (h + 1) * HALF)
-                mx(scores[n][:, cols], query_mx[n], slice(0, P), keys_mx, cols)
+        first_halves = [psum.tile([P, HALF], F32, name=f"scores0{h}") for h in range(2)]
+        for h in range(2):
+            mx(first_halves[h][:], query_mx[0], slice(0, P), keys_mx[h], slice(0, HALF))
+        scores1 = psum.tile([P, I], F32, name="scores1")
+        for h in range(2):
+            mx(scores1[:, h * HALF : (h + 1) * HALF], query_mx[1], slice(0, P), keys_mx[h], slice(0, HALF))
 
-        neg_max = [sb(f"neg_max{n}", [P, 1], F32) for n in range(Q_TILES)]
+        inv_grouped = sb("inv_grouped", [P, PACK, P, PACK], BF16)
+
+        def pool_copy(out, in_):
+            nc.gpsimd.tensor_scalar(out=out, in0=in_, scalar1=1.0, scalar2=0.0, op0=ALU.mult, op1=ALU.add)
+
+        def group_inv(copy, start, width):
+            copy(
+                out=inv_grouped[:, :, start // PACK : (start + width) // PACK, :].rearrange("p t m r -> p m t r"),
+                in_=inv_raw[:, :, start : start + width].rearrange("p r (m t) -> p m t r", t=PACK),
+            )
+
+        neg_half_max = sb("neg_half_max", [P, 1], F32)
+        neg_max = [sb("neg_max0", [P, 1], F32), sb("neg_max1", [P, 1], F32, tag="neg_half_max")]
         row_sum = [sb(f"row_sum{n}", [P, 1], F32) for n in range(Q_TILES)]
         row_rcp = [sb(f"row_rcp{n}", [P, 1], F32) for n in range(Q_TILES)]
         probs = [sb(f"probs{n}", [P, I], F32) for n in range(Q_TILES)]
-        for n in range(Q_TILES):
-            nc.vector.tensor_reduce(out=neg_max[n][:], in_=scores[n][:], axis=AXIS_X, op=ALU.max, negate=True)
-        for n in range(Q_TILES):
-            nc.scalar.activation(
-                out=probs[n][:].rearrange("p (u s e) -> p u s e", u=2, e=2),
-                in_=scores[n][:].rearrange("p (s u e) -> p u s e", u=2, e=2),
-                func=ACT.Exp,
-                bias=neg_max[n][:],
-                accum_out=row_sum[n][:],
+        neg_scores = sb("neg_scores", [P, 2, 2, HALF // PACK, 2], F32)
+        for h in range(2):
+            nc.vector.tensor_scalar(
+                out=neg_scores[:, :, h, :, :],
+                in0=first_halves[h][:].rearrange("p (s u e) -> p u s e", u=2, e=2),
+                scalar1=-1.0,
+                scalar2=neg_half_max[:] if h else None,
+                op0=ALU.mult,
+                op1=ALU.min,
+                accum_out=neg_max[0][:] if h else neg_half_max[:],
             )
-
-        inv_grouped = sb("inv_grouped", [P, PACK, P, PACK], BF16)
-        half_m = HALF // PACK
-        nc.scalar.copy(
-            out=inv_grouped[:, :, 0:half_m, :].rearrange("p t m r -> p m t r"),
-            in_=inv_raw[0][:].rearrange("p r (m t) -> p m t r", t=PACK),
+        nc.vector.tensor_reduce(out=neg_max[1][:], in_=scores1[:], axis=AXIS_X, op=ALU.max, negate=True)
+        nc.scalar.activation(
+            out=probs[0][:],
+            in_=neg_scores[:].rearrange("p u h s e -> p (u h s e)"),
+            func=ACT.Exp,
+            scale=-1.0,
+            bias=neg_max[0][:],
+            accum_out=row_sum[0][:],
         )
-        nc.vector.tensor_copy(
-            out=inv_grouped[:, :, half_m : 2 * half_m, :].rearrange("p t m r -> p m t r"),
-            in_=inv_raw[1][:].rearrange("p r (m t) -> p m t r", t=PACK),
+        nc.scalar.activation(
+            out=probs[1][:].rearrange("p (u s e) -> p u s e", u=2, e=2),
+            in_=scores1[:].rearrange("p (s u e) -> p u s e", u=2, e=2),
+            func=ACT.Exp,
+            bias=neg_max[1][:],
+            accum_out=row_sum[1][:],
         )
 
-        weights = [sb(f"weights{n}", [P, I], BF16) for n in range(Q_TILES)]
+        weights = [[sb(f"weights{n}{u}", [P, HALF], BF16) for u in range(2)] for n in range(Q_TILES)]
         for n in range(Q_TILES):
             nc.vector.reciprocal(out=row_rcp[n][:], in_=row_sum[n][:])
-            nc.vector.scalar_tensor_tensor(
-                out=weights[n][:],
-                in0=probs[n][:],
-                scalar=row_rcp[n][:],
-                in1=gain_wide[:].rearrange("p u s e -> p (u s e)"),
-                op0=ALU.mult,
-                op1=ALU.mult,
-            )
-        inv_mx = quantize("inv", inv_grouped[:].rearrange("p t m r -> p (t m r)"), J)
+            for u in range(2):
+                nc.vector.scalar_tensor_tensor(
+                    out=weights[n][u][:].rearrange("p (s e) -> p s e", e=2),
+                    in0=probs[n][:, u * HALF : (u + 1) * HALF].rearrange("p (s e) -> p s e", e=2),
+                    scalar=row_rcp[n][:],
+                    in1=gain_bank[:, 2 * u : 2 * u + 2, :].rearrange("p e s -> p s e"),
+                    op0=ALU.mult,
+                    op1=ALU.mult,
+                )
+        for start in range(0, 384, 128):
+            group_inv(pool_copy, start, 128)
+        group_inv(nc.scalar.copy, 384, 128)
+        inv_mx = [quantize(f"inv{t}", inv_grouped[:, t, :, :].rearrange("p m r -> p (m r)"), P) for t in range(PACK)]
 
         turned = [psum.tile([P, 2, P], F32, name=f"turned{n}") for n in range(Q_TILES)]
         ft_grouped = [sb(f"ft_grouped{n}", [P, P * PACK], BF16) for n in range(Q_TILES)]
         for n in range(Q_TILES):
-            pairs = weights[n][:].bitcast(F32)
             for u in range(2):
-                nc.tensor.transpose(turned[n][:, u, :], pairs[:, u * P : (u + 1) * P], ident[:])
+                nc.tensor.transpose(turned[n][:, u, :], weights[n][u][:].bitcast(F32), ident[:])
             nc.scalar.copy(
                 out=ft_grouped[n][:].bitcast(F32).rearrange("p (q u) -> p q u", u=2),
                 in_=turned[n][:].rearrange("p u q -> p q u"),
             )
         ft_mx = [quantize(f"ft{n}", ft_grouped[n][:], P) for n in range(Q_TILES)]
 
-        read_grouped = [sb(f"read_grouped{h}", [P, HALF, PACK], BF16) for h in range(2)]
-        nc.scalar.copy(out=read_grouped[0][:], in_=read_raw[0][:].rearrange("p t e -> p e t"))
-        nc.vector.tensor_copy(out=read_grouped[1][:], in_=read_raw[1][:].rearrange("p t e -> p e t"))
+        read_vector = sb("read_vector", [P, HALF, PACK], BF16, tag="inv_raw")
+        read_early = sb("read_early", [P, P, PACK], BF16)
+        read_late = sb("read_late", [P, P, PACK], BF16, tag="weights11")
+        nc.scalar.copy(out=read_early[:], in_=read_raw[:, :, 0:P].rearrange("p t e -> p e t"))
+        nc.scalar.copy(out=read_late[:], in_=read_raw[:, :, E - P : E].rearrange("p t e -> p e t"))
+        for c in range(0, HALF, 64):
+            nc.vector.tensor_copy(
+                out=read_vector[:, c : c + 64, :], in_=read_raw[:, :, P + c : P + c + 64].rearrange("p t e -> p e t")
+            )
+        read_codes = sb("read_codes", [P, E], U32)
+        read_scales = sb("read_scales", [P, E], U8)
+        read_blocks = [read_early[:], read_vector[:, 0:P, :], read_vector[:, P:HALF, :], read_late[:]]
+        for block, grouped in enumerate(read_blocks):
+            nc.vector.quantize_mx(
+                out=read_codes[:, block * P : (block + 1) * P].bitcast(FP8X4),
+                scales=read_scales[:, block * P : (block + 1) * P],
+                in_=grouped.rearrange("p e t -> p (e t)"),
+            )
+        read_mx = (read_codes, read_scales)
 
-        g_grouped = [sb(f"g_grouped{n}", [P, P, PACK], BF16) for n in range(Q_TILES)]
+        g_both = sb("g_grouped", [P, Q_TILES, P, PACK], BF16, tag="read_raw")
+        g_grouped = [g_both[:, n, :, :] for n in range(Q_TILES)]
         for n in range(Q_TILES):
-            g_bank = psum.tile([P, PACK, P], F32, name=f"scores{n}")
+            g_bank = psum.tile([P, PACK, P], F32, name=f"g_bank{n}")
             for t in range(PACK):
-                mx(g_bank[:, t, :], inv_mx, slice(t * P, (t + 1) * P), ft_mx[n], slice(0, P))
-            nc.scalar.copy(out=g_grouped[n][:], in_=g_bank[:].rearrange("p t q -> p q t"))
-        read_mx = [
-            quantize(f"read{h}", read_grouped[h][:].rearrange("p e t -> p (e t)"), HALF) for h in range(2)
-        ]
-        for n in range(Q_TILES):
-            g_mx = quantize(f"g{n}", g_grouped[n][:].rearrange("p q t -> p (q t)"), P)
-            b_bank = psum.tile([P, E], F32, name=f"b_bank{n}")
-            for h in range(2):
-                cols = slice(h * HALF, (h + 1) * HALF)
-                mx(b_bank[:, cols], g_mx, slice(0, P), read_mx[h], slice(0, HALF))
-            result = sb(f"result{n}", [P, E], F32)
-            nc.vector.tensor_tensor(out=result[:], in0=b_bank[:], in1=res_sb[n][:], op=ALU.add)
-            nc.sync.dma_start(out=out[n * P : (n + 1) * P, :], in_=result[:])
+                mx(g_bank[:, t, :], inv_mx[t], slice(0, P), ft_mx[n], slice(0, P))
+            nc.scalar.copy(out=g_grouped[n], in_=g_bank[:].rearrange("p t q -> p q t"))
+        g_mx = [quantize(f"g{n}", g_grouped[n].rearrange("p q t -> p (q t)"), P) for n in range(Q_TILES)]
+
+        pieces = [(0, 0, 256, "gain_bank"), (0, 256, 256, "scores00"), (1, 0, 256, "scores01"), (1, 256, 128, "scores1"), (1, 384, 128, "turned0")]
+        for n, start, width, bank in pieces:
+            cols = slice(start, start + width)
+            b_bank = psum.tile([P, width], F32, name=bank)
+            mx(b_bank[:], g_mx[n], slice(0, P), read_mx, cols)
+            result = sb(f"result{n}_{start}", [P, width], F32)
+            nc.vector.tensor_tensor(out=result[:], in0=b_bank[:], in1=res_sb[n][:, cols], op=ALU.add)
+            nc.sync.dma_start(out=out[n * P : (n + 1) * P, cols], in_=result[:])

@@ -211,6 +211,9 @@ def tile_attend_nystrom_kernel(tc, query, keys_words, keys_scales, inv, gain, re
             for t in range(PACK):
                 mx(g_bank[:, t, :], inv_mx[t], slice(0, P), ft_mx[n], slice(0, P))
             nc.scalar.copy(out=g_grouped[n], in_=g_bank[:].rearrange("p t q -> p q t"))
+        warm = psum.tile([P, PACK, P], F32, name="turned0")
+        for t in range(PACK):
+            mx(warm[:, t, :], inv_mx[t], slice(0, P), ft_mx[1], slice(0, P))
         g_mx = [quantize(f"g{n}", g_grouped[n].rearrange("p q t -> p (q t)"), P) for n in range(Q_TILES)]
 
         pieces = [(0, 0, 256, "gain_bank"), (0, 256, 256, "scores00"), (1, 0, 256, "scores01"), (1, 256, 128, "scores1"), (1, 384, 128, "turned0")]

from contextlib import ExitStack

import concourse.mybir as mybir
from concourse.masks import make_identity

D, T, I, Q, E, J = 512, 2048, 512, 256, 512, 512
FLOPS = 2 * Q * (D * I + I * J + J * E)

F32 = mybir.dt.float32
BF16 = mybir.dt.bfloat16
I32 = mybir.dt.int32
U32 = mybir.dt.uint32
U16 = mybir.dt.uint16
U8 = mybir.dt.uint8
FP8X4 = mybir.dt.float8_e4m3fn_x4
ALU = mybir.AluOpType
ACT = mybir.ActivationFunctionType
AXIS_X = mybir.AxisListType.X

P = 128
PACK = 4
HALF = 256
Q_TILES = Q // P


def tile_attend_nystrom_kernel(tc, query, keys_words, keys_scales, inv, gain, read, res, offs, out):
    nc = tc.nc

    with ExitStack() as ctx:
        keep = ctx.enter_context(tc.tile_pool(name="keep", bufs=1))
        psum = ctx.enter_context(tc.psum_pool(name="psum", bufs=1))

        def sb(name, shape, dtype, tag=None):
            return keep.tile(shape, dtype, name=name, tag=tag or name, align_bytes=64)

        def quantize(name, grouped, width):
            codes = sb(name + "_codes", [P, width], U32)
            scales = sb(name + "_scales", [P, width], U8)
            for c in range(0, width, P):
                nc.vector.quantize_mx(
                    out=codes[:, c : c + P].bitcast(FP8X4),
                    scales=scales[:, c : c + P],
                    in_=grouped[:, PACK * c : PACK * (c + P)],
                )
            return codes, scales

        def mx(dst, stat, stat_cols, mov, mov_cols):
            nc.tensor.matmul_mx(
                out=dst,
                lhsT=stat[0][:, stat_cols].bitcast(FP8X4),
                lhsT_scale=stat[1][:, stat_cols],
                rhs=mov[0][:, mov_cols].bitcast(FP8X4),
                rhs_scale=mov[1][:, mov_cols],
                start=True,
                stop=True,
            )

        offsets = keep.tile([P, I // 16], U16, name="offsets")
        nc.sync.dma_start(offsets[:], offs)
        gain_cols = sb("gain_cols", [P, PACK], F32)
        nc.scalar.dma_start(out=gain_cols[:], in_=gain.rearrange("o (s r) -> (o s) r", r=PACK))

        word_rows = keys_words[0].rearrange("p n t -> p (n t)").bitcast(I32)

        def load_rows(name, matrix):
            tile = sb(name, [P, PACK, matrix.shape[1]], F32)
            nc.sync.dma_start(out=tile[:], in_=matrix.rearrange("(p t) c -> p t c", t=PACK))
            return tile

        pool_words = sb("pool_words", [P, T], U32)
        pool_scales = sb("pool_scales", [P, T], U8)
        ident = sb("ident", [P, P], F32)
        nc.vector.memset(pool_scales[:].bitcast(I32), 0)
        make_identity(nc, ident[:])

        query_raw = load_rows("query_raw", query)
        scale_rows = keys_scales[0].rearrange("(c f) n -> f c n", f=4)
        for f in range(4):
            nc.sync.dma_start(out=pool_scales[f:P:32, :].bitcast(I32), in_=scale_rows[f].bitcast(I32))
        nc.sync.dma_start(out=pool_words[:].bitcast(I32), in_=word_rows)
        inv_raw = load_rows("inv_raw", inv)
        read_raw = load_rows("read_raw", read)
        res_sb = []
        for n in range(Q_TILES):
            tile = sb(f"res{n}", [P, E], F32)
            nc.sync.dma_start(out=tile[:], in_=res[n * P : (n + 1) * P, :])
            res_sb.append(tile)

        gain_bank = psum.tile([P, PACK, P], F32, name="gain_bank")
        for r in range(PACK):
            nc.tensor.transpose(gain_bank[:, r, :], gain_cols[:, r : r + 1].to_broadcast([P, P]), ident[:])

        query_grouped = [sb("query_grouped0", [P, P, PACK], BF16), sb("query_grouped1", [P, P, PACK], BF16)]
        nc.vector.tensor_copy(out=query_grouped[0][:], in_=query_raw[:, :, 0:P].rearrange("p t q -> p q t"))
        nc.scalar.activation(out=query_grouped[1][:], in_=query_raw[:, :, P:Q].rearrange("p t q -> p q t"), func=ACT.Copy)
        key_scales = sb("key_scales", [P, I], U8)
        nc.vector.tensor_copy(key_scales[:], pool_scales[:].indirect(offsets[:]))
        query_mx = [quantize("query0", query_grouped[0][:].rearrange("p q t -> p (q t)"), P)]
        key_words = [sb(f"key_words{h}", [P, HALF], U32) for h in range(2)]
        for h in range(2):
            nc.vector.tensor_copy(
                key_words[h][:],
                pool_words[:].indirect(offsets[:, h * (HALF // 16) : (h + 1) * (HALF // 16)]),
            )
        keys_mx = [(key_words[h], key_scales[:, h * HALF : (h + 1) * HALF]) for h in range(2)]
        query_mx.append(quantize("query1", query_grouped[1][:].rearrange("p q t -> p (q t)"), P))

        first_halves = [psum.tile([P, HALF], F32, name=f"scores0{h}") for h in range(2)]
        for h in range(2):
            mx(first_halves[h][:], query_mx[0], slice(0, P), keys_mx[h], slice(0, HALF))
        scores1 = psum.tile([P, I], F32, name="scores1")
        for h in range(2):
            mx(scores1[:, h * HALF : (h + 1) * HALF], query_mx[1], slice(0, P), keys_mx[h], slice(0, HALF))

        inv_grouped = sb("inv_grouped", [P, PACK, P, PACK], BF16)

        def pool_copy(out, in_):
            nc.gpsimd.tensor_scalar(out=out, in0=in_, scalar1=1.0, scalar2=0.0, op0=ALU.mult, op1=ALU.add)

        def group_inv(copy, start, width):
            copy(
                out=inv_grouped[:, :, start // PACK : (start + width) // PACK, :].rearrange("p t m r -> p m t r"),
                in_=inv_raw[:, :, start : start + width].rearrange("p r (m t) -> p m t r", t=PACK),
            )

        neg_half_max = sb("neg_half_max", [P, 1], F32)
        neg_max = [sb("neg_max0", [P, 1], F32), sb("neg_max1", [P, 1], F32, tag="neg_half_max")]
        row_sum = [sb(f"row_sum{n}", [P, 1], F32) for n in range(Q_TILES)]
        row_rcp = [sb(f"row_rcp{n}", [P, 1], F32) for n in range(Q_TILES)]
        probs = [sb(f"probs{n}", [P, I], F32) for n in range(Q_TILES)]
        neg_scores = sb("neg_scores", [P, 2, 2, HALF // PACK, 2], F32)
        for h in range(2):
            nc.vector.tensor_scalar(
                out=neg_scores[:, :, h, :, :],
                in0=first_halves[h][:].rearrange("p (s u e) -> p u s e", u=2, e=2),
                scalar1=-1.0,
                scalar2=neg_half_max[:] if h else None,
                op0=ALU.mult,
                op1=ALU.min,
                accum_out=neg_max[0][:] if h else neg_half_max[:],
            )
        nc.vector.tensor_reduce(out=neg_max[1][:], in_=scores1[:], axis=AXIS_X, op=ALU.max, negate=True)
        nc.scalar.activation(
            out=probs[0][:],
            in_=neg_scores[:].rearrange("p u h s e -> p (u h s e)"),
            func=ACT.Exp,
            scale=-1.0,
            bias=neg_max[0][:],
            accum_out=row_sum[0][:],
        )
        nc.scalar.activation(
            out=probs[1][:].rearrange("p (u s e) -> p u s e", u=2, e=2),
            in_=scores1[:].rearrange("p (s u e) -> p u s e", u=2, e=2),
            func=ACT.Exp,
            bias=neg_max[1][:],
            accum_out=row_sum[1][:],
        )

        weights = [[sb(f"weights{n}{u}", [P, HALF], BF16) for u in range(2)] for n in range(Q_TILES)]
        for n in range(Q_TILES):
            nc.vector.reciprocal(out=row_rcp[n][:], in_=row_sum[n][:])
            for u in range(2):
                nc.vector.scalar_tensor_tensor(
                    out=weights[n][u][:].rearrange("p (s e) -> p s e", e=2),
                    in0=probs[n][:, u * HALF : (u + 1) * HALF].rearrange("p (s e) -> p s e", e=2),
                    scalar=row_rcp[n][:],
                    in1=gain_bank[:, 2 * u : 2 * u + 2, :].rearrange("p e s -> p s e"),
                    op0=ALU.mult,
                    op1=ALU.mult,
                )
        for start in range(0, 384, 128):
            group_inv(pool_copy, start, 128)
        group_inv(nc.scalar.copy, 384, 128)
        inv_mx = [quantize(f"inv{t}", inv_grouped[:, t, :, :].rearrange("p m r -> p (m r)"), P) for t in range(PACK)]

        turned = [psum.tile([P, 2, P], F32, name=f"turned{n}") for n in range(Q_TILES)]
        ft_grouped = [sb(f"ft_grouped{n}", [P, P * PACK], BF16) for n in range(Q_TILES)]
        for n in range(Q_TILES):
            for u in range(2):
                nc.tensor.transpose(turned[n][:, u, :], weights[n][u][:].bitcast(F32), ident[:])
            nc.scalar.copy(
                out=ft_grouped[n][:].bitcast(F32).rearrange("p (q u) -> p q u", u=2),
                in_=turned[n][:].rearrange("p u q -> p q u"),
            )
        ft_mx = [quantize(f"ft{n}", ft_grouped[n][:], P) for n in range(Q_TILES)]

        read_vector = sb("read_vector", [P, HALF, PACK], BF16, tag="inv_raw")
        read_early = sb("read_early", [P, P, PACK], BF16)
        read_late = sb("read_late", [P, P, PACK], BF16, tag="weights11")
        nc.scalar.copy(out=read_early[:], in_=read_raw[:, :, 0:P].rearrange("p t e -> p e t"))
        nc.scalar.copy(out=read_late[:], in_=read_raw[:, :, E - P : E].rearrange("p t e -> p e t"))
        for c in range(0, HALF, 64):
            nc.vector.tensor_copy(
                out=read_vector[:, c : c + 64, :], in_=read_raw[:, :, P + c : P + c + 64].rearrange("p t e -> p e t")
            )
        read_codes = sb("read_codes", [P, E], U32)
        read_scales = sb("read_scales", [P, E], U8)
        read_blocks = [read_early[:], read_vector[:, 0:P, :], read_vector[:, P:HALF, :], read_late[:]]
        for block, grouped in enumerate(read_blocks):
            nc.vector.quantize_mx(
                out=read_codes[:, block * P : (block + 1) * P].bitcast(FP8X4),
                scales=read_scales[:, block * P : (block + 1) * P],
                in_=grouped.rearrange("p e t -> p (e t)"),
            )
        read_mx = (read_codes, read_scales)

        g_both = sb("g_grouped", [P, Q_TILES, P, PACK], BF16, tag="read_raw")
        g_grouped = [g_both[:, n, :, :] for n in range(Q_TILES)]
        for n in range(Q_TILES):
            g_bank = psum.tile([P, PACK, P], F32, name=f"g_bank{n}")
            for t in range(PACK):
                mx(g_bank[:, t, :], inv_mx[t], slice(0, P), ft_mx[n], slice(0, P))
            nc.scalar.copy(out=g_grouped[n], in_=g_bank[:].rearrange("p t q -> p q t"))
        warm = psum.tile([P, PACK, P], F32, name="turned0")
        for t in range(PACK):
            mx(warm[:, t, :], inv_mx[t], slice(0, P), ft_mx[1], slice(0, P))
        g_mx = [quantize(f"g{n}", g_grouped[n].rearrange("p q t -> p (q t)"), P) for n in range(Q_TILES)]

        pieces = [(0, 0, 256, "gain_bank"), (0, 256, 256, "scores00"), (1, 0, 256, "scores01"), (1, 256, 128, "scores1"), (1, 384, 128, "turned0")]
        for n, start, width, bank in pieces:
            cols = slice(start, start + width)
            b_bank = psum.tile([P, width], F32, name=bank)
            mx(b_bank[:], g_mx[n], slice(0, P), read_mx, cols)
            result = sb(f"result{n}_{start}", [P, width], F32)
            nc.vector.tensor_tensor(out=result[:], in0=b_bank[:], in1=res_sb[n][:, cols], op=ALU.add)
            nc.sync.dma_start(out=out[n * P : (n + 1) * P, cols], in_=result[:])
